import numpy as np
import ml_dtypes


def mxq(x, axis, fmt="e4m3"):
    dtype, down = {"e4m3": (ml_dtypes.float8_e4m3fn, 7), "e5m2": (ml_dtypes.float8_e5m2, 14)}[fmt]
    v = np.moveaxis(np.asarray(x, np.float32).astype(ml_dtypes.bfloat16).astype(np.float64), axis, -1)
    blocks = v.reshape(v.shape[:-1] + (-1, 32))
    amax = np.abs(blocks).max(-1, keepdims=True)
    byte = np.maximum(np.where(amax > 0, np.frexp(amax)[1] - 1 + 127, 0) - down, 1)
    scale = np.exp2(byte - 127.0)
    codes = (blocks / scale).astype(np.float32).astype(dtype).astype(np.float64)
    return np.moveaxis((codes * scale).reshape(v.shape), -1, axis)


WIDE = False


def mx_kscale(k):
    if not WIDE:
        return np.ones(k)
    levels = np.array([10, -10, 5, -5, 0])
    if k % 512:
        return np.exp2(np.random.permutation(np.resize(levels, k // 32))).repeat(32)
    a = np.empty((k // 512, 16))
    for p in range(k // 512):
        a[p, :8] = np.random.permutation(np.resize(levels, 8))
        for g in range(8):
            far = levels[np.abs(levels - a[p, g]) >= 10]
            a[p, g + 8] = far[np.random.randint(len(far))]
    return np.exp2(a.ravel()).repeat(32)


def f64(x):
    return np.asarray(x).astype(np.float64)


def striped(idx):
    return np.tile(np.asarray(idx).reshape(-1, 16).T, (8, 1)).astype(np.uint16)


def unstriped(offs):
    return offs[:16].T.reshape(-1).astype(np.int64)


def striped8(idx):
    return np.asarray(idx).reshape(8, -1, 16).transpose(0, 2, 1).reshape(128, -1).astype(np.uint16)


def unstriped8(offs):
    return offs.reshape(8, 16, -1).transpose(0, 2, 1).reshape(8, -1).astype(np.int64)


def pick8(x, idx, run):
    r = np.arange(len(x))
    return x[r[:, None], idx[r % (8 * run) // run]]


E2M1 = np.array([0.0, 0.5, 1.0, 1.5, 2.0, 3.0, 4.0, 6.0, -0.0, -0.5, -1.0, -1.5, -2.0, -3.0, -4.0, -6.0])


def pack_weight(w, fmt):
    k, n = w.shape
    w = f64(np.asarray(w, np.float32).astype(ml_dtypes.bfloat16)).reshape(k // 32, 32, n)
    amax = np.abs(w).max(1)
    if fmt == "e4m3":
        byte = np.frexp(amax)[1] - 1 + 127 - 7
    else:
        mant, ex = np.frexp(amax / 6.0)
        byte = np.where(mant > 0.5, ex, ex - 1) + 127
    byte = np.clip(np.where(amax > 0, byte, 1), 1, 254)
    scaled = (w * np.exp2(127.0 - byte)[:, None, :]).reshape(k, n).astype(np.float32)
    by_word = np.ascontiguousarray(scaled.reshape(k // 512, 128, 4, n).transpose(0, 1, 3, 2))
    if fmt == "e4m3":
        words = by_word.astype(ml_dtypes.float8_e4m3fn).view(np.uint8)
    else:
        c = by_word.astype(ml_dtypes.float4_e2m1fn).view(np.uint8) & 0xF
        words = (c[..., 0::2] | (c[..., 1::2] << 4)).reshape(k // 512, 128, 2 * n)
    return np.ascontiguousarray(words), np.ascontiguousarray(byte.astype(np.uint8).reshape(k // 512, 16, n))


def unpack_weight(words, scales, fmt):
    g, _, n = scales.shape
    words = np.ascontiguousarray(words).reshape(g, 128, n, -1)
    if fmt == "e4m3":
        vals = words.view(ml_dtypes.float8_e4m3fn).astype(np.float64)
    else:
        nib = np.empty((g, 128, n, 4), np.uint8)
        nib[..., 0::2] = words & 0xF
        nib[..., 1::2] = words >> 4
        vals = E2M1[nib]
    vals = vals * np.repeat(np.exp2(scales.astype(np.float64) - 127.0), 8, axis=1)[..., None]
    return vals.transpose(0, 1, 3, 2).reshape(g * 512, n)


K, J, R, T, Z, M, C, O, N = 512, 256, 512, 1024, 512, 1024, 512, 128, 256


def setup_inputs():
    n = np.random.standard_normal
    idx = np.stack([np.random.permutation(T)[:J] for _ in range(8)])
    idx2 = np.stack([np.random.permutation(T)[:J] for _ in range(8)])
    idx3 = np.random.permutation(M)[:J]
    idx4 = np.stack([np.random.permutation(C)[:J] for _ in range(8)])
    idx5 = np.random.permutation(C)[:J]
    idx6 = np.random.permutation(C)[:O]
    idx7 = np.stack([np.random.permutation(C)[:O] for _ in range(8)])
    fk = mx_kscale(K)
    fr = mx_kscale(R)
    fz = mx_kscale(Z)
    wp = pack_weight(n((K, R)) * 1 / np.sqrt(K) / fk[:, None] * fr, "e4m3")
    xop = pack_weight(n((Z, M)) / fz[:, None], "e4m3")
    w2p = pack_weight(n((Z, R)) * 1 / np.sqrt(Z) * fz[:, None] * fr, "e2m1")
    wbp = pack_weight(n((R, N)) * 1 / np.sqrt(R) / fr[:, None], "e2m1")
    return {
        "ta": (np.random.randint(-7, 8, (K, T)).astype(np.float64)).astype(np.float32),
        "ga": ((np.random.randint(10, 25, (K, 1)) / 64.0) * fk[:, None]).astype(np.float32),
        "gb": ((np.random.randint(4, 13, (K, 1)) / 64.0) * fk[:, None]).astype(np.float32),
        "w_words": wp[0],
        "w_scales": wp[1],
        "xo_words": xop[0],
        "xo_scales": xop[1],
        "w2_words": w2p[0],
        "w2_scales": w2p[1],
        "sa": (np.random.uniform(0.5, 1.6, (R, 1))).astype(np.float32),
        "sb": (np.random.uniform(0.5, 1.6, (R, 1))).astype(np.float32),
        "wb_words": wbp[0],
        "wb_scales": wbp[1],
        "offs": striped8(idx),
        "offs2": striped8(idx2),
        "offs3": striped(idx3),
        "offs4": striped8(idx4),
        "offs5": striped(idx5),
        "offs6": striped(idx6),
        "offs7": striped8(idx7),
    }


def reference(ta, ga, gb, w_words, w_scales, xo_words, xo_scales, w2_words, w2_scales, sa, sb, wb_words, wb_scales, offs, offs2, offs3, offs4, offs5, offs6, offs7):
    idx = unstriped8(offs)
    idx2 = unstriped8(offs2)
    idx3 = unstriped(offs3)
    idx4 = unstriped8(offs4)
    idx5 = unstriped(offs5)
    idx6 = unstriped(offs6)
    idx7 = unstriped8(offs7)
    wu = unpack_weight(w_words, w_scales, "e4m3")
    xou = unpack_weight(xo_words, xo_scales, "e4m3")
    w2u = unpack_weight(w2_words, w2_scales, "e2m1")
    wbu = unpack_weight(wb_words, wb_scales, "e2m1")
    xc = pick8(f64(ta), idx, 64) * f64(ga) + pick8(f64(ta), idx2, 64) * f64(gb)
    xcq = mxq(xc, 0, "e4m3")
    a = wu.T @ xcq
    xoidx3g = xou[:, idx3]
    b = w2u.T @ xoidx3g
    pw = np.zeros((R, C))
    pw[np.arange(R)[:, None], idx4[np.arange(R) % 512 // 64]] = a
    pv = np.zeros((R, C))
    pv[:, idx5] = b
    pg = pw + pv
    hid = np.maximum(pg[:, idx6] * f64(sa), pick8(pg, idx7, 64) * f64(sb))
    hidq = mxq(hid, 0, "e4m3")
    y = wbu.T @ hidq
    return y

@@ -1,0 +1,240 @@
+from contextlib import ExitStack
+
+import concourse.mybir as mybir
+
+K, J, R, T, Z, M, C, O, N = 512, 256, 512, 1024, 512, 1024, 512, 128, 256
+FLOPS = 2 * (K * R * J + Z * R * J + R * N * O)
+
+F32 = mybir.dt.float32
+BF16 = mybir.dt.bfloat16
+I32 = mybir.dt.int32
+U32 = mybir.dt.uint32
+U16 = mybir.dt.uint16
+U8 = mybir.dt.uint8
+FP8X4 = mybir.dt.float8_e4m3fn_x4
+FP4X4 = mybir.dt.float4_e2m1fn_x4
+COPY = mybir.ActivationFunctionType.Copy
+ADD = mybir.AluOpType.add
+MAX = mybir.AluOpType.max
+
+P = 128
+PACK = 4
+QUADS = 4
+
+
+def tile_picked_refined_plain_two_twoposts_one_plain_kernel(
+    tc, ta, ga, gb, w_words, w_scales, xo_words, xo_scales, w2_words, w2_scales, sa, sb,
+    wb_words, wb_scales, offs, offs2, offs3, offs4, offs5, offs6, offs7, out,
+):
+    nc = tc.nc
+    with ExitStack() as ctx:
+        lists = ctx.enter_context(tc.tile_pool(name="lists", bufs=1))
+        keep = ctx.enter_context(tc.tile_pool(name="keep", bufs=1))
+        psum = ctx.enter_context(tc.psum_pool(name="psum", bufs=1))
+
+        def load_list(src, name):
+            tile = lists.tile(list(src.shape), U16, name=name)
+            nc.sync.dma_start(tile[:], src)
+            return tile
+
+        def load_scale_rows(queue, src, name):
+            width = src.shape[2]
+            staged = keep.tile([PACK, QUADS, width // 4], I32, name=name)
+            queue.dma_start(staged[:], src[0].rearrange("(q r) n -> r q n", r=PACK).bitcast(I32))
+            return staged
+
+        def zeroed_plane(width, name):
+            plane = keep.tile([P, width], U8, name=name, align_bytes=64)
+            nc.vector.memset(plane[:].bitcast(I32), 0)
+            return plane
+
+        def spread_scale_rows(plane, staged):
+            for q in range(QUADS):
+                nc.vector.tensor_copy(plane[32 * q : 32 * q + PACK, :].bitcast(I32), staged[:, q, :])
+
+        def load_plane(plane, src):
+            for q in range(QUADS):
+                nc.sync.dma_start(plane[32 * q : 32 * q + PACK, :].bitcast(I32), src[0, PACK * q : PACK * (q + 1), :].bitcast(I32))
+
+        def load_column(src, name):
+            tile = keep.tile([P, PACK], F32, name=name)
+            nc.sync.dma_start(tile[:], src.rearrange("(p t) o -> p (t o)", t=PACK))
+            return tile
+
+        def deal(copy, dst, src):
+            copy(dst, src.rearrange("p (m t) -> p t m", t=PACK))
+
+        ta_rows = ta.rearrange("(p t) c -> p t c", t=PACK)
+        ta_sb = [keep.tile([P, T], F32, name=f"ta{t}", tag=f"ta{t}") for t in range(PACK)]
+
+        w2_plane = zeroed_plane(R, "w2_plane")
+        xo_plane = zeroed_plane(M, "xo_plane")
+        w_plane = zeroed_plane(R, "w_plane")
+        wb_plane = zeroed_plane(N, "wb_plane")
+        pv = [keep.tile([P, C], F32, name=f"pv{t}", tag=f"pv{t}") for t in range(PACK)]
+        pw = [keep.tile([P, C], F32, name=f"pw{t}") for t in range(PACK)]
+        for t in range(PACK):
+            nc.vector.memset(pv[t][:], 0.0)
+            nc.gpsimd.memset(pw[t][:], 0.0)
+
+        w2_sc_staged = load_scale_rows(nc.sync, w2_scales, "w2_sc_staged")
+        xo_sc_staged = load_scale_rows(nc.sync, xo_scales, "xo_sc_staged")
+        idx = load_list(offs, "idx")
+        ga_sb = load_column(ga, "ga_sb")
+        nc.sync.dma_start(ta_sb[0][:], ta_rows[:, 0, :])
+        idx2 = load_list(offs2, "idx2")
+        gb_sb = load_column(gb, "gb_sb")
+        nc.sync.dma_start(ta_sb[1][:], ta_rows[:, 1, :])
+        idx3 = load_list(offs3, "idx3")
+        w2_raw = keep.tile([P, 2 * R], U8, name="w2_raw")
+        nc.sync.dma_start(w2_raw[:].bitcast(I32), w2_words[0].bitcast(I32))
+        xo_sb = keep.tile([P, M], I32, name="xo_sb", tag="xo_sb", align_bytes=64)
+        nc.sync.dma_start(xo_sb[:], xo_words[0].rearrange("p n t -> p (n t)").bitcast(I32))
+        idx5 = load_list(offs5, "idx5")
+        for t in range(2, PACK):
+            nc.sync.dma_start(ta_sb[t][:], ta_rows[:, t, :])
+        load_plane(w_plane, w_scales)
+        w_raw = keep.tile([P, R], I32, name="w_raw")
+        nc.sync.dma_start(w_raw[:], w_words[0].rearrange("p n t -> p (n t)").bitcast(I32))
+        idx6 = load_list(offs6, "idx6")
+        idx7 = load_list(offs7, "idx7")
+        sa_sb = load_column(sa, "sa_sb")
+        sb_sb = load_column(sb, "sb_sb")
+        idx4 = load_list(offs4, "idx4")
+        wb_sb = keep.tile([P, 2 * N], U8, name="wb_sb", align_bytes=64)
+        nc.sync.dma_start(wb_sb[:].bitcast(I32), wb_words[0].bitcast(I32))
+        load_plane(wb_plane, wb_scales)
+
+        spread_scale_rows(w2_plane, w2_sc_staged)
+        w2_sc = keep.tile([P, PACK, P], U8, name="w2_sc", align_bytes=64)
+        deal(nc.gpsimd.tensor_copy, w2_sc[:], w2_plane[:])
+        spread_scale_rows(xo_plane, xo_sc_staged)
+        xo_sc = keep.tile([P, J], U8, name="xo_sc", align_bytes=64)
+        nc.vector.tensor_copy(xo_sc[:], xo_plane[:].indirect(idx3[:]))
+        xo_picked = keep.tile([P, J], U32, name="xo_picked", align_bytes=64)
+        nc.vector.tensor_copy(xo_picked[:], xo_sb[:].bitcast(U32).indirect(idx3[:]))
+        w2_sb = keep.tile([P, PACK, 2 * P], U8, name="w2_sb", align_bytes=64)
+        nc.gpsimd.tensor_copy(w2_sb[:].rearrange("p t (m e) -> p t m e", e=2), w2_raw[:].rearrange("p (m t e) -> p t m e", t=PACK, e=2))
+        w_sc = keep.tile([P, PACK, P], U8, name="w_sc", align_bytes=64)
+        deal(nc.gpsimd.tensor_copy, w_sc[:], w_plane[:])
+
+        def notes_product(t, bank):
+            nc.tensor.matmul_mx(bank[:, t % 2, :], w2_sb[:, t, :].bitcast(FP4X4), w2_sc[:, t, :],
+                                xo_picked[:].bitcast(FP8X4), xo_sc[:], start=True, stop=True)
+
+        b01_ps = psum.tile([P, 2, J], F32, name="b01_ps")
+        notes_product(0, b01_ps)
+        notes_product(1, b01_ps)
+        b0_sb = keep.tile([P, J], F32, name="b0_sb")
+        nc.vector.tensor_copy(b0_sb[:], b01_ps[:, 0, :])
+        nc.vector.tensor_copy(pv[0][:].indirect(idx5[:]), b0_sb[:])
+
+        coarse = [keep.tile([P, 2, J], F32, name=f"coarse{u}") for u in range(2)]
+        fine = [keep.tile([P, 2, J], F32, name=f"fine{u}") for u in range(2)]
+        xc = keep.tile([P, J, PACK], BF16, name="xc", tag="xo_sb", align_bytes=64)
+
+        def fetch_codes(t):
+            nc.scalar.activation(coarse[t // 2][:, t % 2, :], ta_sb[t][:].indirect(idx[:]), COPY, scale=ga_sb[:, t : t + 1])
+            nc.scalar.activation(fine[t // 2][:, t % 2, :], ta_sb[t][:].indirect(idx2[:]), COPY, scale=gb_sb[:, t : t + 1])
+
+        def add_codes(u, cols):
+            nc.vector.tensor_tensor(xc[:, cols, 2 * u : 2 * u + 2], coarse[u][:, :, cols].rearrange("p t j -> p j t"),
+                                    fine[u][:, :, cols].rearrange("p t j -> p j t"), ADD)
+
+        xc_codes = keep.tile([P, J], U32, name="xc_codes", align_bytes=64)
+        xc_sc = keep.tile([P, J], U8, name="xc_sc", align_bytes=64)
+
+        def quantize_codes(cols):
+            nc.vector.quantize_mx(xc_codes[:, cols].bitcast(FP8X4), xc_sc[:, cols], xc[:, cols, :].rearrange("p j t -> p (j t)"))
+
+        whole = slice(0, J)
+        halves = [slice(0, J // 2), slice(J // 2, J)]
+        fetch_codes(0)
+        fetch_codes(1)
+        add_codes(0, whole)
+        fetch_codes(2)
+        fetch_codes(3)
+        for cols in halves:
+            add_codes(1, cols)
+        for cols in halves:
+            quantize_codes(cols)
+
+        w_sb = keep.tile([P, PACK, P], U32, name="w_sb", align_bytes=64)
+        deal(nc.gpsimd.tensor_copy, w_sb[:], w_raw[:].bitcast(U32))
+
+        def first_product(t, cols, bank):
+            nc.tensor.matmul_mx(bank, w_sb[:, t, :].bitcast(FP8X4), w_sc[:, t, :],
+                                xc_codes[:, cols].bitcast(FP8X4), xc_sc[:, cols], start=True, stop=True)
+
+        a0_ps = [psum.tile([P, J // 2], F32, name=f"a0_ps{h}") for h in range(2)]
+        for h in range(2):
+            first_product(0, halves[h], a0_ps[h][:])
+        a_ps = [None] + [psum.tile([P, J], F32, name=f"a_ps{t}", tag=f"a_ps{t}") for t in range(1, PACK)]
+        for t in range(1, PACK):
+            first_product(t, whole, a_ps[t][:])
+
+        b23_sb = keep.tile([P, 2, J], F32, name="b23_sb")
+        a_sb = [keep.tile([P, J], F32, name=f"a_sb{t}") for t in range(PACK)]
+        pg = [keep.tile([P, C], F32, name=f"pg{t}", tag=f"pg{t}" if t < 3 else "pv2") for t in range(PACK)]
+        first = [keep.tile([P, 2, O], F32, name=f"first{u}") for u in range(2)]
+        second = [keep.tile([P, 2, O], F32, name=f"second{u}") for u in range(2)]
+        hid = keep.tile([P, O, PACK], BF16, name="hid", align_bytes=64)
+
+        def put_b(t, src):
+            nc.scalar.activation(pv[t][:].indirect(idx5[:]), src, COPY)
+
+        def put_a(t, cols):
+            nc.vector.tensor_copy(pw[t][:].indirect(idx4[:, cols.start // 16 : cols.stop // 16]), a_sb[t][:, cols])
+
+        def add_boards(t, engine):
+            engine.tensor_tensor(pg[t][:], pw[t][:], pv[t][:], ADD)
+
+        def read_board(t):
+            nc.scalar.activation(first[t // 2][:, t % 2, :], pg[t][:].indirect(idx6[:]), COPY, scale=sa_sb[:, t : t + 1])
+            nc.scalar.activation(second[t // 2][:, t % 2, :], pg[t][:].indirect(idx7[:]), COPY, scale=sb_sb[:, t : t + 1])
+
+        def larger(u):
+            nc.vector.tensor_tensor(hid[:, :, 2 * u : 2 * u + 2], first[u][:].rearrange("p t o -> p o t"),
+                                    second[u][:].rearrange("p t o -> p o t"), MAX)
+
+        b1_sb = keep.tile([P, J], F32, name="b1_sb", tag="ta3")
+        nc.scalar.copy(b1_sb[:], b01_ps[:, 1, :])
+        put_b(1, b1_sb[:])
+        nc.vector.tensor_copy(a_sb[0][:, halves[0]], a0_ps[0][:])
+        nc.scalar.copy(a_sb[0][:, halves[1]], a0_ps[1][:])
+        for t in range(1, PACK):
+            nc.scalar.copy(a_sb[t][:], a_ps[t][:])
+        b23_ps = psum.tile([P, 2, J], F32, name="b23_ps", tag="a_ps1")
+        notes_product(2, b23_ps)
+        notes_product(3, b23_ps)
+        nc.scalar.copy(b23_sb[:], b23_ps[:])
+        put_b(2, b23_sb[:, 0, :])
+        put_b(3, b23_sb[:, 1, :])
+        put_a(0, halves[0])
+        put_a(0, halves[1])
+        put_a(1, whole)
+        add_boards(0, nc.gpsimd)
+        add_boards(1, nc.gpsimd)
+        read_board(0)
+        read_board(1)
+        put_a(2, whole)
+        add_boards(2, nc.gpsimd)
+        read_board(2)
+        put_a(3, whole)
+        add_boards(3, nc.vector)
+        read_board(3)
+        larger(0)
+        larger(1)
+        hid_codes = keep.tile([P, O], U32, name="hid_codes", align_bytes=64)
+        hid_sc = keep.tile([P, O], U8, name="hid_sc", align_bytes=64)
+        nc.vector.quantize_mx(hid_codes[:].bitcast(FP8X4), hid_sc[:], hid[:].rearrange("p o t -> p (o t)"))
+
+        y_ps = [psum.tile([P, O], F32, name=f"y_ps{c}", tag=f"a_ps{2 + c}") for c in range(2)]
+        y_sb = [keep.tile([P, O], F32, name=f"y_sb{c}") for c in range(2)]
+        for c in range(2):
+            nc.tensor.matmul_mx(y_ps[c][:], wb_sb[:, 2 * P * c : 2 * P * (c + 1)].bitcast(FP4X4), wb_plane[:, P * c : P * (c + 1)],
+                                hid_codes[:].bitcast(FP8X4), hid_sc[:], start=True, stop=True)
+        nc.vector.tensor_copy(y_sb[0][:], y_ps[0][:])
+        nc.sync.dma_start(out[0:P, :], y_sb[0][:])
+        nc.scalar.copy(y_sb[1][:], y_ps[1][:])
+        nc.scalar.dma_start(out[P : 2 * P, :], y_sb[1][:])

@@ -37,11 +37,8 @@ def tile_picked_refined_plain_two_twoposts_one_plain_kernel(
             nc.sync.dma_start(tile[:], src)
             return tile
 
-        def load_scale_rows(queue, src, name):
-            width = src.shape[2]
-            staged = keep.tile([PACK, QUADS, width // 4], I32, name=name)
-            queue.dma_start(staged[:], src[0].rearrange("(q r) n -> r q n", r=PACK).bitcast(I32))
-            return staged
+        def stage_scale_rows(staged, src):
+            nc.sync.dma_start(staged.bitcast(I32), src[0].rearrange("(q r) n -> r q n", r=PACK).bitcast(I32))
 
         def zeroed_plane(width, name):
             plane = keep.tile([P, width], U8, name=name, align_bytes=64)
@@ -50,7 +47,7 @@ def tile_picked_refined_plain_two_twoposts_one_plain_kernel(
 
         def spread_scale_rows(plane, staged):
             for q in range(QUADS):
-                nc.vector.tensor_copy(plane[32 * q : 32 * q + PACK, :].bitcast(I32), staged[:, q, :])
+                nc.vector.tensor_copy(plane[32 * q : 32 * q + PACK, :].bitcast(I32), staged[:, q, :].bitcast(I32))
 
         def load_plane(plane, src):
             for q in range(QUADS):
@@ -67,9 +64,13 @@ def tile_picked_refined_plain_two_twoposts_one_plain_kernel(
         ta_rows = ta.rearrange("(p t) c -> p t c", t=PACK)
         ta_sb = [keep.tile([P, T], F32, name=f"ta{t}", tag=f"ta{t}") for t in range(PACK)]
 
-        w2_plane = zeroed_plane(R, "w2_plane")
+        warm_in = keep.tile([P, 1], F32, name="warm_in")
+        warm_out = keep.tile([P, 1], F32, name="warm_out")
+        nc.gpsimd.memset(warm_in[:], 0.0)
+        nc.scalar.activation(warm_out[:], warm_in[:], COPY)
+
         xo_plane = zeroed_plane(M, "xo_plane")
-        w_plane = zeroed_plane(R, "w_plane")
+        ww_plane = zeroed_plane(2 * R, "ww_plane")
         wb_plane = zeroed_plane(N, "wb_plane")
         pv = [keep.tile([P, C], F32, name=f"pv{t}", tag=f"pv{t}") for t in range(PACK)]
         pw = [keep.tile([P, C], F32, name=f"pw{t}") for t in range(PACK)]
@@ -77,14 +78,17 @@ def tile_picked_refined_plain_two_twoposts_one_plain_kernel(
             nc.vector.memset(pv[t][:], 0.0)
             nc.gpsimd.memset(pw[t][:], 0.0)
 
-        w2_sc_staged = load_scale_rows(nc.sync, w2_scales, "w2_sc_staged")
-        xo_sc_staged = load_scale_rows(nc.sync, xo_scales, "xo_sc_staged")
         idx = load_list(offs, "idx")
         ga_sb = load_column(ga, "ga_sb")
         nc.sync.dma_start(ta_sb[0][:], ta_rows[:, 0, :])
         idx2 = load_list(offs2, "idx2")
         gb_sb = load_column(gb, "gb_sb")
         nc.sync.dma_start(ta_sb[1][:], ta_rows[:, 1, :])
+        ww_staged = keep.tile([PACK, QUADS, 2 * R], U8, name="ww_staged")
+        stage_scale_rows(ww_staged[:, :, 0:R], w2_scales)
+        stage_scale_rows(ww_staged[:, :, R : 2 * R], w_scales)
+        xo_staged = keep.tile([PACK, QUADS, M], U8, name="xo_staged")
+        stage_scale_rows(xo_staged[:], xo_scales)
         idx3 = load_list(offs3, "idx3")
         w2_raw = keep.tile([P, 2 * R], U8, name="w2_raw")
         nc.sync.dma_start(w2_raw[:].bitcast(I32), w2_words[0].bitcast(I32))
@@ -93,8 +97,7 @@ def tile_picked_refined_plain_two_twoposts_one_plain_kernel(
         idx5 = load_list(offs5, "idx5")
         for t in range(2, PACK):
             nc.sync.dma_start(ta_sb[t][:], ta_rows[:, t, :])
-        load_plane(w_plane, w_scales)
-        w_raw = keep.tile([P, R], I32, name="w_raw")
+        w_raw = keep.tile([P, R], I32, name="w_raw", tag="w_raw")
         nc.sync.dma_start(w_raw[:], w_words[0].rearrange("p n t -> p (n t)").bitcast(I32))
         idx6 = load_list(offs6, "idx6")
         idx7 = load_list(offs7, "idx7")
@@ -105,18 +108,17 @@ def tile_picked_refined_plain_two_twoposts_one_plain_kernel(
         nc.sync.dma_start(wb_sb[:].bitcast(I32), wb_words[0].bitcast(I32))
         load_plane(wb_plane, wb_scales)
 
-        spread_scale_rows(w2_plane, w2_sc_staged)
-        w2_sc = keep.tile([P, PACK, P], U8, name="w2_sc", align_bytes=64)
-        deal(nc.gpsimd.tensor_copy, w2_sc[:], w2_plane[:])
-        spread_scale_rows(xo_plane, xo_sc_staged)
+        spread_scale_rows(ww_plane, ww_staged)
+        spread_scale_rows(xo_plane, xo_staged)
+        ww_sc = keep.tile([P, 2, PACK, P], U8, name="ww_sc", align_bytes=64)
+        nc.vector.tensor_copy(ww_sc[:], ww_plane[:].rearrange("p (s m t) -> p s t m", s=2, t=PACK))
+        w2_sc, w_sc = ww_sc[:, 0], ww_sc[:, 1]
         xo_sc = keep.tile([P, J], U8, name="xo_sc", align_bytes=64)
         nc.vector.tensor_copy(xo_sc[:], xo_plane[:].indirect(idx3[:]))
         xo_picked = keep.tile([P, J], U32, name="xo_picked", align_bytes=64)
         nc.vector.tensor_copy(xo_picked[:], xo_sb[:].bitcast(U32).indirect(idx3[:]))
         w2_sb = keep.tile([P, PACK, 2 * P], U8, name="w2_sb", align_bytes=64)
-        nc.gpsimd.tensor_copy(w2_sb[:].rearrange("p t (m e) -> p t m e", e=2), w2_raw[:].rearrange("p (m t e) -> p t m e", t=PACK, e=2))
-        w_sc = keep.tile([P, PACK, P], U8, name="w_sc", align_bytes=64)
-        deal(nc.gpsimd.tensor_copy, w_sc[:], w_plane[:])
+        deal(nc.scalar.copy, w2_sb[:].bitcast(U16), w2_raw[:].bitcast(U16))
 
         def notes_product(t, bank):
             nc.tensor.matmul_mx(bank[:, t % 2, :], w2_sb[:, t, :].bitcast(FP4X4), w2_sc[:, t, :],
@@ -160,7 +162,7 @@ def tile_picked_refined_plain_two_twoposts_one_plain_kernel(
             quantize_codes(cols)
 
         w_sb = keep.tile([P, PACK, P], U32, name="w_sb", align_bytes=64)
-        deal(nc.gpsimd.tensor_copy, w_sb[:], w_raw[:].bitcast(U32))
+        deal(nc.scalar.copy, w_sb[:], w_raw[:].bitcast(U32))
 
         def first_product(t, cols, bank):
             nc.tensor.matmul_mx(bank, w_sb[:, t, :].bitcast(FP8X4), w_sc[:, t, :],
@@ -175,7 +177,7 @@ def tile_picked_refined_plain_two_twoposts_one_plain_kernel(
 
         b23_sb = keep.tile([P, 2, J], F32, name="b23_sb")
         a_sb = [keep.tile([P, J], F32, name=f"a_sb{t}") for t in range(PACK)]
-        pg = [keep.tile([P, C], F32, name=f"pg{t}", tag=f"pg{t}" if t < 3 else "pv2") for t in range(PACK)]
+        pg = [keep.tile([P, C], F32, name=f"pg{t}") for t in range(PACK)]
         first = [keep.tile([P, 2, O], F32, name=f"first{u}") for u in range(2)]
         second = [keep.tile([P, 2, O], F32, name=f"second{u}") for u in range(2)]
         hid = keep.tile([P, O, PACK], BF16, name="hid", align_bytes=64)
@@ -197,7 +199,7 @@ def tile_picked_refined_plain_two_twoposts_one_plain_kernel(
             nc.vector.tensor_tensor(hid[:, :, 2 * u : 2 * u + 2], first[u][:].rearrange("p t o -> p o t"),
                                     second[u][:].rearrange("p t o -> p o t"), MAX)
 
-        b1_sb = keep.tile([P, J], F32, name="b1_sb", tag="ta3")
+        b1_sb = keep.tile([P, J], F32, name="b1_sb", tag="w_raw")
         nc.scalar.copy(b1_sb[:], b01_ps[:, 1, :])
         put_b(1, b1_sb[:])
         nc.vector.tensor_copy(a_sb[0][:, halves[0]], a0_ps[0][:])
@@ -211,14 +213,14 @@ def tile_picked_refined_plain_two_twoposts_one_plain_kernel(
         put_b(2, b23_sb[:, 0, :])
         put_b(3, b23_sb[:, 1, :])
         put_a(0, halves[0])
-        put_a(0, halves[1])
         put_a(1, whole)
-        add_boards(0, nc.gpsimd)
-        add_boards(1, nc.gpsimd)
-        read_board(0)
+        put_a(0, halves[1])
+        add_boards(1, nc.vector)
+        add_boards(0, nc.vector)
         read_board(1)
+        read_board(0)
         put_a(2, whole)
-        add_boards(2, nc.gpsimd)
+        add_boards(2, nc.vector)
         read_board(2)
         put_a(3, whole)
         add_boards(3, nc.vector)

@@ -37,8 +37,11 @@ def tile_picked_refined_plain_two_twoposts_one_plain_kernel(
             nc.sync.dma_start(tile[:], src)
             return tile
 
-        def stage_scale_rows(staged, src):
-            nc.sync.dma_start(staged.bitcast(I32), src[0].rearrange("(q r) n -> r q n", r=PACK).bitcast(I32))
+        def load_scale_rows(queue, src, name):
+            width = src.shape[2]
+            staged = keep.tile([PACK, QUADS, width // 4], I32, name=name)
+            queue.dma_start(staged[:], src[0].rearrange("(q r) n -> r q n", r=PACK).bitcast(I32))
+            return staged
 
         def zeroed_plane(width, name):
             plane = keep.tile([P, width], U8, name=name, align_bytes=64)
@@ -47,7 +50,7 @@ def tile_picked_refined_plain_two_twoposts_one_plain_kernel(
 
         def spread_scale_rows(plane, staged):
             for q in range(QUADS):
-                nc.vector.tensor_copy(plane[32 * q : 32 * q + PACK, :].bitcast(I32), staged[:, q, :].bitcast(I32))
+                nc.vector.tensor_copy(plane[32 * q : 32 * q + PACK, :].bitcast(I32), staged[:, q, :])
 
         def load_plane(plane, src):
             for q in range(QUADS):
@@ -62,15 +65,16 @@ def tile_picked_refined_plain_two_twoposts_one_plain_kernel(
             copy(dst, src.rearrange("p (m t) -> p t m", t=PACK))
 
         ta_rows = ta.rearrange("(p t) c -> p t c", t=PACK)
-        ta_sb = [keep.tile([P, T], F32, name=f"ta{t}", tag=f"ta{t}") for t in range(PACK)]
+        ta_sb = [keep.tile([P, T], F32, name=f"ta{t}") for t in range(PACK)]
 
         warm_in = keep.tile([P, 1], F32, name="warm_in")
         warm_out = keep.tile([P, 1], F32, name="warm_out")
         nc.gpsimd.memset(warm_in[:], 0.0)
         nc.scalar.activation(warm_out[:], warm_in[:], COPY)
 
+        w2_plane = zeroed_plane(R, "w2_plane")
         xo_plane = zeroed_plane(M, "xo_plane")
-        ww_plane = zeroed_plane(2 * R, "ww_plane")
+        w_plane = zeroed_plane(R, "w_plane")
         wb_plane = zeroed_plane(N, "wb_plane")
         pv = [keep.tile([P, C], F32, name=f"pv{t}", tag=f"pv{t}") for t in range(PACK)]
         pw = [keep.tile([P, C], F32, name=f"pw{t}") for t in range(PACK)]
@@ -78,25 +82,22 @@ def tile_picked_refined_plain_two_twoposts_one_plain_kernel(
             nc.vector.memset(pv[t][:], 0.0)
             nc.gpsimd.memset(pw[t][:], 0.0)
 
+        w2_sc_staged = load_scale_rows(nc.sync, w2_scales, "w2_sc_staged")
+        xo_sc_staged = load_scale_rows(nc.sync, xo_scales, "xo_sc_staged")
+        idx3 = load_list(offs3, "idx3")
         idx = load_list(offs, "idx")
         ga_sb = load_column(ga, "ga_sb")
         nc.sync.dma_start(ta_sb[0][:], ta_rows[:, 0, :])
-        idx2 = load_list(offs2, "idx2")
-        gb_sb = load_column(gb, "gb_sb")
-        nc.sync.dma_start(ta_sb[1][:], ta_rows[:, 1, :])
-        ww_staged = keep.tile([PACK, QUADS, 2 * R], U8, name="ww_staged")
-        stage_scale_rows(ww_staged[:, :, 0:R], w2_scales)
-        stage_scale_rows(ww_staged[:, :, R : 2 * R], w_scales)
-        xo_staged = keep.tile([PACK, QUADS, M], U8, name="xo_staged")
-        stage_scale_rows(xo_staged[:], xo_scales)
-        idx3 = load_list(offs3, "idx3")
         w2_raw = keep.tile([P, 2 * R], U8, name="w2_raw")
         nc.sync.dma_start(w2_raw[:].bitcast(I32), w2_words[0].bitcast(I32))
-        xo_sb = keep.tile([P, M], I32, name="xo_sb", tag="xo_sb", align_bytes=64)
+        xo_sb = keep.tile([P, M], I32, name="xo_sb")
         nc.sync.dma_start(xo_sb[:], xo_words[0].rearrange("p n t -> p (n t)").bitcast(I32))
+        idx2 = load_list(offs2, "idx2")
+        gb_sb = load_column(gb, "gb_sb")
         idx5 = load_list(offs5, "idx5")
-        for t in range(2, PACK):
+        for t in range(1, PACK):
             nc.sync.dma_start(ta_sb[t][:], ta_rows[:, t, :])
+        load_plane(w_plane, w_scales)
         w_raw = keep.tile([P, R], I32, name="w_raw", tag="w_raw")
         nc.sync.dma_start(w_raw[:], w_words[0].rearrange("p n t -> p (n t)").bitcast(I32))
         idx6 = load_list(offs6, "idx6")
@@ -108,17 +109,18 @@ def tile_picked_refined_plain_two_twoposts_one_plain_kernel(
         nc.sync.dma_start(wb_sb[:].bitcast(I32), wb_words[0].bitcast(I32))
         load_plane(wb_plane, wb_scales)
 
-        spread_scale_rows(ww_plane, ww_staged)
-        spread_scale_rows(xo_plane, xo_staged)
-        ww_sc = keep.tile([P, 2, PACK, P], U8, name="ww_sc", align_bytes=64)
-        nc.vector.tensor_copy(ww_sc[:], ww_plane[:].rearrange("p (s m t) -> p s t m", s=2, t=PACK))
-        w2_sc, w_sc = ww_sc[:, 0], ww_sc[:, 1]
+        spread_scale_rows(w2_plane, w2_sc_staged)
+        w2_sc = keep.tile([P, PACK, P], U8, name="w2_sc", align_bytes=64)
+        deal(nc.gpsimd.tensor_copy, w2_sc[:], w2_plane[:])
+        spread_scale_rows(xo_plane, xo_sc_staged)
         xo_sc = keep.tile([P, J], U8, name="xo_sc", align_bytes=64)
         nc.vector.tensor_copy(xo_sc[:], xo_plane[:].indirect(idx3[:]))
         xo_picked = keep.tile([P, J], U32, name="xo_picked", align_bytes=64)
         nc.vector.tensor_copy(xo_picked[:], xo_sb[:].bitcast(U32).indirect(idx3[:]))
         w2_sb = keep.tile([P, PACK, 2 * P], U8, name="w2_sb", align_bytes=64)
-        deal(nc.scalar.copy, w2_sb[:].bitcast(U16), w2_raw[:].bitcast(U16))
+        nc.gpsimd.tensor_copy(w2_sb[:].rearrange("p t (m e) -> p t m e", e=2), w2_raw[:].rearrange("p (m t e) -> p t m e", t=PACK, e=2))
+        w_sc = keep.tile([P, PACK, P], U8, name="w_sc", align_bytes=64)
+        deal(nc.gpsimd.tensor_copy, w_sc[:], w_plane[:])
 
         def notes_product(t, bank):
             nc.tensor.matmul_mx(bank[:, t % 2, :], w2_sb[:, t, :].bitcast(FP4X4), w2_sc[:, t, :],
@@ -133,7 +135,7 @@ def tile_picked_refined_plain_two_twoposts_one_plain_kernel(
 
         coarse = [keep.tile([P, 2, J], F32, name=f"coarse{u}") for u in range(2)]
         fine = [keep.tile([P, 2, J], F32, name=f"fine{u}") for u in range(2)]
-        xc = keep.tile([P, J, PACK], BF16, name="xc", tag="xo_sb", align_bytes=64)
+        xc = keep.tile([P, J, PACK], BF16, name="xc", align_bytes=64)
 
         def fetch_codes(t):
             nc.scalar.activation(coarse[t // 2][:, t % 2, :], ta_sb[t][:].indirect(idx[:]), COPY, scale=ga_sb[:, t : t + 1])
@@ -162,22 +164,21 @@ def tile_picked_refined_plain_two_twoposts_one_plain_kernel(
             quantize_codes(cols)
 
         w_sb = keep.tile([P, PACK, P], U32, name="w_sb", align_bytes=64)
-        deal(nc.scalar.copy, w_sb[:], w_raw[:].bitcast(U32))
+        nc.scalar.copy(w_sb[:].rearrange("p t m -> p m t"), w_raw[:].bitcast(U32).rearrange("p (m t) -> p m t", t=PACK))
 
         def first_product(t, cols, bank):
             nc.tensor.matmul_mx(bank, w_sb[:, t, :].bitcast(FP8X4), w_sc[:, t, :],
                                 xc_codes[:, cols].bitcast(FP8X4), xc_sc[:, cols], start=True, stop=True)
 
-        a0_ps = [psum.tile([P, J // 2], F32, name=f"a0_ps{h}") for h in range(2)]
-        for h in range(2):
-            first_product(0, halves[h], a0_ps[h][:])
-        a_ps = [None] + [psum.tile([P, J], F32, name=f"a_ps{t}", tag=f"a_ps{t}") for t in range(1, PACK)]
+        a_ps = [psum.tile([P, J], F32, name=f"a_ps{t}", tag=f"a_ps{t}") for t in range(PACK)]
+        for cols in halves:
+            first_product(0, cols, a_ps[0][:, cols])
         for t in range(1, PACK):
             first_product(t, whole, a_ps[t][:])
 
         b23_sb = keep.tile([P, 2, J], F32, name="b23_sb")
         a_sb = [keep.tile([P, J], F32, name=f"a_sb{t}") for t in range(PACK)]
-        pg = [keep.tile([P, C], F32, name=f"pg{t}") for t in range(PACK)]
+        pg = [keep.tile([P, C], F32, name=f"pg{t}", tag=f"pg{t}" if t < 3 else "pv2") for t in range(PACK)]
         first = [keep.tile([P, 2, O], F32, name=f"first{u}") for u in range(2)]
         second = [keep.tile([P, 2, O], F32, name=f"second{u}") for u in range(2)]
         hid = keep.tile([P, O, PACK], BF16, name="hid", align_bytes=64)
@@ -202,8 +203,7 @@ def tile_picked_refined_plain_two_twoposts_one_plain_kernel(
         b1_sb = keep.tile([P, J], F32, name="b1_sb", tag="w_raw")
         nc.scalar.copy(b1_sb[:], b01_ps[:, 1, :])
         put_b(1, b1_sb[:])
-        nc.vector.tensor_copy(a_sb[0][:, halves[0]], a0_ps[0][:])
-        nc.scalar.copy(a_sb[0][:, halves[1]], a0_ps[1][:])
+        nc.vector.tensor_copy(a_sb[0][:], a_ps[0][:])
         for t in range(1, PACK):
             nc.scalar.copy(a_sb[t][:], a_ps[t][:])
         b23_ps = psum.tile([P, 2, J], F32, name="b23_ps", tag="a_ps1")
@@ -212,15 +212,14 @@ def tile_picked_refined_plain_two_twoposts_one_plain_kernel(
         nc.scalar.copy(b23_sb[:], b23_ps[:])
         put_b(2, b23_sb[:, 0, :])
         put_b(3, b23_sb[:, 1, :])
-        put_a(0, halves[0])
+        put_a(0, whole)
         put_a(1, whole)
-        put_a(0, halves[1])
-        add_boards(1, nc.vector)
-        add_boards(0, nc.vector)
-        read_board(1)
+        add_boards(0, nc.gpsimd)
+        add_boards(1, nc.gpsimd)
         read_board(0)
+        read_board(1)
         put_a(2, whole)
-        add_boards(2, nc.vector)
+        add_boards(2, nc.gpsimd)
         read_board(2)
         put_a(3, whole)
         add_boards(3, nc.vector)

@@ -39,12 +39,12 @@ def tile_picked_refined_plain_two_twoposts_one_plain_kernel(
 
         def load_scale_rows(queue, src, name):
             width = src.shape[2]
-            staged = keep.tile([PACK, QUADS, width // 4], I32, name=name)
+            staged = keep.tile([PACK, QUADS, width // 4], I32, name=name, tag=name, align_bytes=64)
             queue.dma_start(staged[:], src[0].rearrange("(q r) n -> r q n", r=PACK).bitcast(I32))
             return staged
 
         def zeroed_plane(width, name):
-            plane = keep.tile([P, width], U8, name=name, align_bytes=64)
+            plane = keep.tile([P, width], U8, name=name, tag=name, align_bytes=64)
             nc.vector.memset(plane[:].bitcast(I32), 0)
             return plane
 
@@ -76,25 +76,23 @@ def tile_picked_refined_plain_two_twoposts_one_plain_kernel(
         xo_plane = zeroed_plane(M, "xo_plane")
         w_plane = zeroed_plane(R, "w_plane")
         wb_plane = zeroed_plane(N, "wb_plane")
-        pv = [keep.tile([P, C], F32, name=f"pv{t}", tag=f"pv{t}") for t in range(PACK)]
-        pw = [keep.tile([P, C], F32, name=f"pw{t}") for t in range(PACK)]
-        for t in range(PACK):
-            nc.vector.memset(pv[t][:], 0.0)
-            nc.gpsimd.memset(pw[t][:], 0.0)
+        pv = [keep.tile([P, C], F32, name=f"pv{t}") for t in range(2)]
+        for board in pv:
+            nc.vector.memset(board[:].bitcast(I32), 0)
 
         w2_sc_staged = load_scale_rows(nc.sync, w2_scales, "w2_sc_staged")
         xo_sc_staged = load_scale_rows(nc.sync, xo_scales, "xo_sc_staged")
         idx3 = load_list(offs3, "idx3")
+        idx5 = load_list(offs5, "idx5")
+        w2_raw = keep.tile([P, 2 * R], U8, name="w2_raw", tag="w2_raw", align_bytes=64)
+        nc.sync.dma_start(w2_raw[:].bitcast(I32), w2_words[0].bitcast(I32))
+        xo_sb = keep.tile([P, M], I32, name="xo_sb", tag="xo_sb", align_bytes=64)
+        nc.sync.dma_start(xo_sb[:], xo_words[0].rearrange("p n t -> p (n t)").bitcast(I32))
+        nc.sync.dma_start(ta_sb[0][:], ta_rows[:, 0, :])
         idx = load_list(offs, "idx")
         ga_sb = load_column(ga, "ga_sb")
-        nc.sync.dma_start(ta_sb[0][:], ta_rows[:, 0, :])
-        w2_raw = keep.tile([P, 2 * R], U8, name="w2_raw")
-        nc.sync.dma_start(w2_raw[:].bitcast(I32), w2_words[0].bitcast(I32))
-        xo_sb = keep.tile([P, M], I32, name="xo_sb")
-        nc.sync.dma_start(xo_sb[:], xo_words[0].rearrange("p n t -> p (n t)").bitcast(I32))
         idx2 = load_list(offs2, "idx2")
         gb_sb = load_column(gb, "gb_sb")
-        idx5 = load_list(offs5, "idx5")
         for t in range(1, PACK):
             nc.sync.dma_start(ta_sb[t][:], ta_rows[:, t, :])
         load_plane(w_plane, w_scales)
@@ -118,20 +116,30 @@ def tile_picked_refined_plain_two_twoposts_one_plain_kernel(
         xo_picked = keep.tile([P, J], U32, name="xo_picked", align_bytes=64)
         nc.vector.tensor_copy(xo_picked[:], xo_sb[:].bitcast(U32).indirect(idx3[:]))
         w2_sb = keep.tile([P, PACK, 2 * P], U8, name="w2_sb", align_bytes=64)
-        nc.gpsimd.tensor_copy(w2_sb[:].rearrange("p t (m e) -> p t m e", e=2), w2_raw[:].rearrange("p (m t e) -> p t m e", t=PACK, e=2))
+        nc.scalar.copy(w2_sb[:].bitcast(U16).rearrange("p t m -> p m t"), w2_raw[:].bitcast(U16).rearrange("p (m t) -> p m t", t=PACK))
+
+        def late_board(name, tag):
+            board = keep.tile([P, C], F32, name=name, tag=tag, align_bytes=64)
+            nc.gpsimd.memset(board[:], 0.0)
+            return board
+
+        pv = pv + [late_board("pv2", "w2_sc_staged"), late_board("pv3", "xo_sc_staged")]
+        pw = [late_board(f"pw{t}", tag) for t, tag in enumerate(["w2_raw", "w2_plane", "xo_plane", "xo_sb"])]
         w_sc = keep.tile([P, PACK, P], U8, name="w_sc", align_bytes=64)
         deal(nc.gpsimd.tensor_copy, w_sc[:], w_plane[:])
 
         def notes_product(t, bank):
-            nc.tensor.matmul_mx(bank[:, t % 2, :], w2_sb[:, t, :].bitcast(FP4X4), w2_sc[:, t, :],
+            nc.tensor.matmul_mx(bank, w2_sb[:, t, :].bitcast(FP4X4), w2_sc[:, t, :],
                                 xo_picked[:].bitcast(FP8X4), xo_sc[:], start=True, stop=True)
 
-        b01_ps = psum.tile([P, 2, J], F32, name="b01_ps")
-        notes_product(0, b01_ps)
-        notes_product(1, b01_ps)
-        b0_sb = keep.tile([P, J], F32, name="b0_sb")
-        nc.vector.tensor_copy(b0_sb[:], b01_ps[:, 0, :])
-        nc.vector.tensor_copy(pv[0][:].indirect(idx5[:]), b0_sb[:])
+        b_ps = [psum.tile([P, J], F32, name=f"b_ps{t}") for t in range(3)]
+        for t in range(3):
+            notes_product(t, b_ps[t][:])
+        b_early = [keep.tile([P, J], F32, name=f"b{t}_sb") for t in range(2)]
+        for t in range(2):
+            nc.vector.tensor_copy(b_early[t][:], b_ps[t][:])
+        for t in range(2):
+            nc.vector.tensor_copy(pv[t][:].indirect(idx5[:]), b_early[t][:])
 
         coarse = [keep.tile([P, 2, J], F32, name=f"coarse{u}") for u in range(2)]
         fine = [keep.tile([P, 2, J], F32, name=f"fine{u}") for u in range(2)]
@@ -170,15 +178,20 @@ def tile_picked_refined_plain_two_twoposts_one_plain_kernel(
             nc.tensor.matmul_mx(bank, w_sb[:, t, :].bitcast(FP8X4), w_sc[:, t, :],
                                 xc_codes[:, cols].bitcast(FP8X4), xc_sc[:, cols], start=True, stop=True)
 
-        a_ps = [psum.tile([P, J], F32, name=f"a_ps{t}", tag=f"a_ps{t}") for t in range(PACK)]
+        a0_ps = psum.tile([P, J], F32, name="a0_ps")
+        a1_ps = psum.tile([P, J], F32, name="a1_ps", tag="a1_ps")
+        a23_ps = psum.tile([P, 2, J], F32, name="a23_ps")
         for cols in halves:
-            first_product(0, cols, a_ps[0][:, cols])
-        for t in range(1, PACK):
-            first_product(t, whole, a_ps[t][:])
+            first_product(0, cols, a0_ps[:, cols])
+        first_product(1, whole, a1_ps[:])
+        first_product(2, whole, a23_ps[:, 0, :])
+        first_product(3, whole, a23_ps[:, 1, :])
 
-        b23_sb = keep.tile([P, 2, J], F32, name="b23_sb")
-        a_sb = [keep.tile([P, J], F32, name=f"a_sb{t}") for t in range(PACK)]
-        pg = [keep.tile([P, C], F32, name=f"pg{t}", tag=f"pg{t}" if t < 3 else "pv2") for t in range(PACK)]
+        a0_sb = keep.tile([P, J], F32, name="a0_sb")
+        a1_sb = keep.tile([P, J], F32, name="a1_sb")
+        a23_sb = keep.tile([P, 2, J], F32, name="a23_sb")
+        a_sb = [a0_sb[:], a1_sb[:], a23_sb[:, 0, :], a23_sb[:, 1, :]]
+        pg = [keep.tile([P, C], F32, name=f"pg{t}", tag=f"pg{t}" if t < 3 else "w2_sc_staged", align_bytes=64) for t in range(PACK)]
         first = [keep.tile([P, 2, O], F32, name=f"first{u}") for u in range(2)]
         second = [keep.tile([P, 2, O], F32, name=f"second{u}") for u in range(2)]
         hid = keep.tile([P, O, PACK], BF16, name="hid", align_bytes=64)
@@ -186,8 +199,8 @@ def tile_picked_refined_plain_two_twoposts_one_plain_kernel(
         def put_b(t, src):
             nc.scalar.activation(pv[t][:].indirect(idx5[:]), src, COPY)
 
-        def put_a(t, cols):
-            nc.vector.tensor_copy(pw[t][:].indirect(idx4[:, cols.start // 16 : cols.stop // 16]), a_sb[t][:, cols])
+        def put_a(t):
+            nc.vector.tensor_copy(pw[t][:].indirect(idx4[:]), a_sb[t])
 
         def add_boards(t, engine):
             engine.tensor_tensor(pg[t][:], pw[t][:], pv[t][:], ADD)
@@ -200,28 +213,27 @@ def tile_picked_refined_plain_two_twoposts_one_plain_kernel(
             nc.vector.tensor_tensor(hid[:, :, 2 * u : 2 * u + 2], first[u][:].rearrange("p t o -> p o t"),
                                     second[u][:].rearrange("p t o -> p o t"), MAX)
 
-        b1_sb = keep.tile([P, J], F32, name="b1_sb", tag="w_raw")
-        nc.scalar.copy(b1_sb[:], b01_ps[:, 1, :])
-        put_b(1, b1_sb[:])
-        nc.vector.tensor_copy(a_sb[0][:], a_ps[0][:])
-        for t in range(1, PACK):
-            nc.scalar.copy(a_sb[t][:], a_ps[t][:])
-        b23_ps = psum.tile([P, 2, J], F32, name="b23_ps", tag="a_ps1")
-        notes_product(2, b23_ps)
-        notes_product(3, b23_ps)
-        nc.scalar.copy(b23_sb[:], b23_ps[:])
-        put_b(2, b23_sb[:, 0, :])
-        put_b(3, b23_sb[:, 1, :])
-        put_a(0, whole)
-        put_a(1, whole)
+        b2_sb = keep.tile([P, J], F32, name="b2_sb", tag="w_raw")
+        nc.scalar.copy(b2_sb[:], b_ps[2][:])
+        put_b(2, b2_sb[:])
+        nc.vector.tensor_copy(a0_sb[:], a0_ps[:])
+        nc.scalar.copy(a1_sb[:], a1_ps[:])
+        nc.scalar.copy(a23_sb[:], a23_ps[:])
+        b3_ps = psum.tile([P, J], F32, name="b3_ps", tag="a1_ps")
+        notes_product(3, b3_ps[:])
+        b3_sb = keep.tile([P, J], F32, name="b3_sb")
+        nc.scalar.copy(b3_sb[:], b3_ps[:])
+        put_b(3, b3_sb[:])
+        put_a(0)
+        put_a(1)
         add_boards(0, nc.gpsimd)
         add_boards(1, nc.gpsimd)
         read_board(0)
         read_board(1)
-        put_a(2, whole)
+        put_a(2)
         add_boards(2, nc.gpsimd)
         read_board(2)
-        put_a(3, whole)
+        put_a(3)
         add_boards(3, nc.vector)
         read_board(3)
         larger(0)
@@ -230,7 +242,7 @@ def tile_picked_refined_plain_two_twoposts_one_plain_kernel(
         hid_sc = keep.tile([P, O], U8, name="hid_sc", align_bytes=64)
         nc.vector.quantize_mx(hid_codes[:].bitcast(FP8X4), hid_sc[:], hid[:].rearrange("p o t -> p (o t)"))
 
-        y_ps = [psum.tile([P, O], F32, name=f"y_ps{c}", tag=f"a_ps{2 + c}") for c in range(2)]
+        y_ps = [psum.tile([P, O], F32, name=f"y_ps{c}") for c in range(2)]
         y_sb = [keep.tile([P, O], F32, name=f"y_sb{c}") for c in range(2)]
         for c in range(2):
             nc.tensor.matmul_mx(y_ps[c][:], wb_sb[:, 2 * P * c : 2 * P * (c + 1)].bitcast(FP4X4), wb_plane[:, P * c : P * (c + 1)],

@@ -67,11 +67,6 @@ def tile_picked_refined_plain_two_twoposts_one_plain_kernel(
         ta_rows = ta.rearrange("(p t) c -> p t c", t=PACK)
         ta_sb = [keep.tile([P, T], F32, name=f"ta{t}") for t in range(PACK)]
 
-        warm_in = keep.tile([P, 1], F32, name="warm_in")
-        warm_out = keep.tile([P, 1], F32, name="warm_out")
-        nc.gpsimd.memset(warm_in[:], 0.0)
-        nc.scalar.activation(warm_out[:], warm_in[:], COPY)
-
         w2_plane = zeroed_plane(R, "w2_plane")
         xo_plane = zeroed_plane(M, "xo_plane")
         w_plane = zeroed_plane(R, "w_plane")

from contextlib import ExitStack

import concourse.mybir as mybir

K, J, R, T, Z, M, C, O, N = 512, 256, 512, 1024, 512, 1024, 512, 128, 256
FLOPS = 2 * (K * R * J + Z * R * J + R * N * O)

F32 = mybir.dt.float32
BF16 = mybir.dt.bfloat16
I32 = mybir.dt.int32
U32 = mybir.dt.uint32
U16 = mybir.dt.uint16
U8 = mybir.dt.uint8
FP8X4 = mybir.dt.float8_e4m3fn_x4
FP4X4 = mybir.dt.float4_e2m1fn_x4
COPY = mybir.ActivationFunctionType.Copy
ADD = mybir.AluOpType.add
MAX = mybir.AluOpType.max

P = 128
PACK = 4
QUADS = 4


def tile_picked_refined_plain_two_twoposts_one_plain_kernel(
    tc, ta, ga, gb, w_words, w_scales, xo_words, xo_scales, w2_words, w2_scales, sa, sb,
    wb_words, wb_scales, offs, offs2, offs3, offs4, offs5, offs6, offs7, out,
):
    nc = tc.nc
    with ExitStack() as ctx:
        lists = ctx.enter_context(tc.tile_pool(name="lists", bufs=1))
        keep = ctx.enter_context(tc.tile_pool(name="keep", bufs=1))
        psum = ctx.enter_context(tc.psum_pool(name="psum", bufs=1))

        def load_list(src, name):
            tile = lists.tile(list(src.shape), U16, name=name)
            nc.sync.dma_start(tile[:], src)
            return tile

        def load_scale_rows(queue, src, name):
            width = src.shape[2]
            staged = keep.tile([PACK, QUADS, width // 4], I32, name=name, tag=name, align_bytes=64)
            queue.dma_start(staged[:], src[0].rearrange("(q r) n -> r q n", r=PACK).bitcast(I32))
            return staged

        def zeroed_plane(width, name):
            plane = keep.tile([P, width], U8, name=name, tag=name, align_bytes=64)
            nc.vector.memset(plane[:].bitcast(I32), 0)
            return plane

        def spread_scale_rows(plane, staged):
            for q in range(QUADS):
                nc.vector.tensor_copy(plane[32 * q : 32 * q + PACK, :].bitcast(I32), staged[:, q, :])

        def load_plane(plane, src):
            for q in range(QUADS):
                nc.sync.dma_start(plane[32 * q : 32 * q + PACK, :].bitcast(I32), src[0, PACK * q : PACK * (q + 1), :].bitcast(I32))

        def load_column(src, name):
            tile = keep.tile([P, PACK], F32, name=name)
            nc.sync.dma_start(tile[:], src.rearrange("(p t) o -> p (t o)", t=PACK))
            return tile

        def deal(copy, dst, src):
            copy(dst, src.rearrange("p (m t) -> p t m", t=PACK))

        ta_rows = ta.rearrange("(p t) c -> p t c", t=PACK)
        ta_sb = [keep.tile([P, T], F32, name=f"ta{t}") for t in range(PACK)]

        w2_plane = zeroed_plane(R, "w2_plane")
        xo_plane = zeroed_plane(M, "xo_plane")
        w_plane = zeroed_plane(R, "w_plane")
        wb_plane = zeroed_plane(N, "wb_plane")
        pv = [keep.tile([P, C], F32, name=f"pv{t}") for t in range(2)]
        for board in pv:
            nc.vector.memset(board[:].bitcast(I32), 0)

        w2_sc_staged = load_scale_rows(nc.sync, w2_scales, "w2_sc_staged")
        xo_sc_staged = load_scale_rows(nc.sync, xo_scales, "xo_sc_staged")
        idx3 = load_list(offs3, "idx3")
        idx5 = load_list(offs5, "idx5")
        w2_raw = keep.tile([P, 2 * R], U8, name="w2_raw", tag="w2_raw", align_bytes=64)
        nc.sync.dma_start(w2_raw[:].bitcast(I32), w2_words[0].bitcast(I32))
        xo_sb = keep.tile([P, M], I32, name="xo_sb", tag="xo_sb", align_bytes=64)
        nc.sync.dma_start(xo_sb[:], xo_words[0].rearrange("p n t -> p (n t)").bitcast(I32))
        nc.sync.dma_start(ta_sb[0][:], ta_rows[:, 0, :])
        idx = load_list(offs, "idx")
        ga_sb = load_column(ga, "ga_sb")
        idx2 = load_list(offs2, "idx2")
        gb_sb = load_column(gb, "gb_sb")
        for t in range(1, PACK):
            nc.sync.dma_start(ta_sb[t][:], ta_rows[:, t, :])
        load_plane(w_plane, w_scales)
        w_raw = keep.tile([P, R], I32, name="w_raw", tag="w_raw")
        nc.sync.dma_start(w_raw[:], w_words[0].rearrange("p n t -> p (n t)").bitcast(I32))
        idx6 = load_list(offs6, "idx6")
        idx7 = load_list(offs7, "idx7")
        sa_sb = load_column(sa, "sa_sb")
        sb_sb = load_column(sb, "sb_sb")
        idx4 = load_list(offs4, "idx4")
        wb_sb = keep.tile([P, 2 * N], U8, name="wb_sb", align_bytes=64)
        nc.sync.dma_start(wb_sb[:].bitcast(I32), wb_words[0].bitcast(I32))
        load_plane(wb_plane, wb_scales)

        spread_scale_rows(w2_plane, w2_sc_staged)
        w2_sc = keep.tile([P, PACK, P], U8, name="w2_sc", align_bytes=64)
        deal(nc.gpsimd.tensor_copy, w2_sc[:], w2_plane[:])
        spread_scale_rows(xo_plane, xo_sc_staged)
        xo_sc = keep.tile([P, J], U8, name="xo_sc", align_bytes=64)
        nc.vector.tensor_copy(xo_sc[:], xo_plane[:].indirect(idx3[:]))
        xo_picked = keep.tile([P, J], U32, name="xo_picked", align_bytes=64)
        nc.vector.tensor_copy(xo_picked[:], xo_sb[:].bitcast(U32).indirect(idx3[:]))
        w2_sb = keep.tile([P, PACK, 2 * P], U8, name="w2_sb", align_bytes=64)
        nc.scalar.copy(w2_sb[:].bitcast(U16).rearrange("p t m -> p m t"), w2_raw[:].bitcast(U16).rearrange("p (m t) -> p m t", t=PACK))

        def late_board(name, tag):
            board = keep.tile([P, C], F32, name=name, tag=tag, align_bytes=64)
            nc.gpsimd.memset(board[:], 0.0)
            return board

        pv = pv + [late_board("pv2", "w2_sc_staged"), late_board("pv3", "xo_sc_staged")]
        pw = [late_board(f"pw{t}", tag) for t, tag in enumerate(["w2_raw", "w2_plane", "xo_plane", "xo_sb"])]
        w_sc = keep.tile([P, PACK, P], U8, name="w_sc", align_bytes=64)
        deal(nc.gpsimd.tensor_copy, w_sc[:], w_plane[:])

        def notes_product(t, bank):
            nc.tensor.matmul_mx(bank, w2_sb[:, t, :].bitcast(FP4X4), w2_sc[:, t, :],
                                xo_picked[:].bitcast(FP8X4), xo_sc[:], start=True, stop=True)

        b_ps = [psum.tile([P, J], F32, name=f"b_ps{t}") for t in range(3)]
        for t in range(3):
            notes_product(t, b_ps[t][:])
        b_early = [keep.tile([P, J], F32, name=f"b{t}_sb") for t in range(2)]
        for t in range(2):
            nc.vector.tensor_copy(b_early[t][:], b_ps[t][:])
        for t in range(2):
            nc.vector.tensor_copy(pv[t][:].indirect(idx5[:]), b_early[t][:])

        coarse = [keep.tile([P, 2, J], F32, name=f"coarse{u}") for u in range(2)]
        fine = [keep.tile([P, 2, J], F32, name=f"fine{u}") for u in range(2)]
        xc = keep.tile([P, J, PACK], BF16, name="xc", align_bytes=64)

        def fetch_codes(t):
            nc.scalar.activation(coarse[t // 2][:, t % 2, :], ta_sb[t][:].indirect(idx[:]), COPY, scale=ga_sb[:, t : t + 1])
            nc.scalar.activation(fine[t // 2][:, t % 2, :], ta_sb[t][:].indirect(idx2[:]), COPY, scale=gb_sb[:, t : t + 1])

        def add_codes(u, cols):
            nc.vector.tensor_tensor(xc[:, cols, 2 * u : 2 * u + 2], coarse[u][:, :, cols].rearrange("p t j -> p j t"),
                                    fine[u][:, :, cols].rearrange("p t j -> p j t"), ADD)

        xc_codes = keep.tile([P, J], U32, name="xc_codes", align_bytes=64)
        xc_sc = keep.tile([P, J], U8, name="xc_sc", align_bytes=64)

        def quantize_codes(cols):
            nc.vector.quantize_mx(xc_codes[:, cols].bitcast(FP8X4), xc_sc[:, cols], xc[:, cols, :].rearrange("p j t -> p (j t)"))

        whole = slice(0, J)
        halves = [slice(0, J // 2), slice(J // 2, J)]
        fetch_codes(0)
        fetch_codes(1)
        add_codes(0, whole)
        fetch_codes(2)
        fetch_codes(3)
        for cols in halves:
            add_codes(1, cols)
        for cols in halves:
            quantize_codes(cols)

        w_sb = keep.tile([P, PACK, P], U32, name="w_sb", align_bytes=64)
        nc.scalar.copy(w_sb[:].rearrange("p t m -> p m t"), w_raw[:].bitcast(U32).rearrange("p (m t) -> p m t", t=PACK))

        def first_product(t, cols, bank):
            nc.tensor.matmul_mx(bank, w_sb[:, t, :].bitcast(FP8X4), w_sc[:, t, :],
                                xc_codes[:, cols].bitcast(FP8X4), xc_sc[:, cols], start=True, stop=True)

        a0_ps = psum.tile([P, J], F32, name="a0_ps")
        a1_ps = psum.tile([P, J], F32, name="a1_ps", tag="a1_ps")
        a23_ps = psum.tile([P, 2, J], F32, name="a23_ps")
        for cols in halves:
            first_product(0, cols, a0_ps[:, cols])
        first_product(1, whole, a1_ps[:])
        first_product(2, whole, a23_ps[:, 0, :])
        first_product(3, whole, a23_ps[:, 1, :])

        a0_sb = keep.tile([P, J], F32, name="a0_sb")
        a1_sb = keep.tile([P, J], F32, name="a1_sb")
        a23_sb = keep.tile([P, 2, J], F32, name="a23_sb")
        a_sb = [a0_sb[:], a1_sb[:], a23_sb[:, 0, :], a23_sb[:, 1, :]]
        pg = [keep.tile([P, C], F32, name=f"pg{t}", tag=f"pg{t}" if t < 3 else "w2_sc_staged", align_bytes=64) for t in range(PACK)]
        first = [keep.tile([P, 2, O], F32, name=f"first{u}") for u in range(2)]
        second = [keep.tile([P, 2, O], F32, name=f"second{u}") for u in range(2)]
        hid = keep.tile([P, O, PACK], BF16, name="hid", align_bytes=64)

        def put_b(t, src):
            nc.scalar.activation(pv[t][:].indirect(idx5[:]), src, COPY)

        def put_a(t):
            nc.vector.tensor_copy(pw[t][:].indirect(idx4[:]), a_sb[t])

        def add_boards(t, engine):
            engine.tensor_tensor(pg[t][:], pw[t][:], pv[t][:], ADD)

        def read_board(t):
            nc.scalar.activation(first[t // 2][:, t % 2, :], pg[t][:].indirect(idx6[:]), COPY, scale=sa_sb[:, t : t + 1])
            nc.scalar.activation(second[t // 2][:, t % 2, :], pg[t][:].indirect(idx7[:]), COPY, scale=sb_sb[:, t : t + 1])

        def larger(u):
            nc.vector.tensor_tensor(hid[:, :, 2 * u : 2 * u + 2], first[u][:].rearrange("p t o -> p o t"),
                                    second[u][:].rearrange("p t o -> p o t"), MAX)

        b2_sb = keep.tile([P, J], F32, name="b2_sb", tag="w_raw")
        nc.scalar.copy(b2_sb[:], b_ps[2][:])
        put_b(2, b2_sb[:])
        nc.vector.tensor_copy(a0_sb[:], a0_ps[:])
        nc.scalar.copy(a1_sb[:], a1_ps[:])
        nc.scalar.copy(a23_sb[:], a23_ps[:])
        b3_ps = psum.tile([P, J], F32, name="b3_ps", tag="a1_ps")
        notes_product(3, b3_ps[:])
        b3_sb = keep.tile([P, J], F32, name="b3_sb")
        nc.scalar.copy(b3_sb[:], b3_ps[:])
        put_b(3, b3_sb[:])
        put_a(0)
        put_a(1)
        add_boards(0, nc.gpsimd)
        add_boards(1, nc.gpsimd)
        read_board(0)
        read_board(1)
        put_a(2)
        add_boards(2, nc.gpsimd)
        read_board(2)
        put_a(3)
        add_boards(3, nc.vector)
        read_board(3)
        larger(0)
        larger(1)
        hid_codes = keep.tile([P, O], U32, name="hid_codes", align_bytes=64)
        hid_sc = keep.tile([P, O], U8, name="hid_sc", align_bytes=64)
        nc.vector.quantize_mx(hid_codes[:].bitcast(FP8X4), hid_sc[:], hid[:].rearrange("p o t -> p (o t)"))

        y_ps = [psum.tile([P, O], F32, name=f"y_ps{c}") for c in range(2)]
        y_sb = [keep.tile([P, O], F32, name=f"y_sb{c}") for c in range(2)]
        for c in range(2):
            nc.tensor.matmul_mx(y_ps[c][:], wb_sb[:, 2 * P * c : 2 * P * (c + 1)].bitcast(FP4X4), wb_plane[:, P * c : P * (c + 1)],
                                hid_codes[:].bitcast(FP8X4), hid_sc[:], start=True, stop=True)
        nc.vector.tensor_copy(y_sb[0][:], y_ps[0][:])
        nc.sync.dma_start(out[0:P, :], y_sb[0][:])
        nc.scalar.copy(y_sb[1][:], y_ps[1][:])
        nc.scalar.dma_start(out[P : 2 * P, :], y_sb[1][:])
